import numpy as np
import ml_dtypes


def mxq(x, axis, fmt="e4m3"):
    dtype, down = {"e4m3": (ml_dtypes.float8_e4m3fn, 7), "e5m2": (ml_dtypes.float8_e5m2, 14)}[fmt]
    v = np.moveaxis(np.asarray(x, np.float32).astype(ml_dtypes.bfloat16).astype(np.float64), axis, -1)
    blocks = v.reshape(v.shape[:-1] + (-1, 32))
    amax = np.abs(blocks).max(-1, keepdims=True)
    byte = np.maximum(np.where(amax > 0, np.frexp(amax)[1] - 1 + 127, 0) - down, 1)
    scale = np.exp2(byte - 127.0)
    codes = (blocks / scale).astype(np.float32).astype(dtype).astype(np.float64)
    return np.moveaxis((codes * scale).reshape(v.shape), -1, axis)


WIDE = False


def mx_kscale(k):
    if not WIDE:
        return np.ones(k)
    levels = np.array([10, -10, 5, -5, 0])
    if k % 512:
        return np.exp2(np.random.permutation(np.resize(levels, k // 32))).repeat(32)
    a = np.empty((k // 512, 16))
    for p in range(k // 512):
        a[p, :8] = np.random.permutation(np.resize(levels, 8))
        for g in range(8):
            far = levels[np.abs(levels - a[p, g]) >= 10]
            a[p, g + 8] = far[np.random.randint(len(far))]
    return np.exp2(a.ravel()).repeat(32)


def f64(x):
    return np.asarray(x).astype(np.float64)


def striped(idx):
    return np.tile(idx.reshape(-1, 16).T, (8, 1)).astype(np.uint16)


def unstriped(offs):
    return offs[:16].T.reshape(-1).astype(np.int64)


def striped8(idx):
    return np.concatenate([x.reshape(-1, 16).T for x in idx]).astype(np.uint16)


def runs(offs, k):
    lists = np.stack([offs[16 * r : 16 * r + 16].T.reshape(-1) for r in range(8)]).astype(np.int64)
    return lists[np.arange(k) % 512 // 64]


def pack_weight(w):
    k, n = w.shape
    w = f64(np.asarray(w, np.float32).astype(ml_dtypes.bfloat16)).reshape(k // 32, 32, n)
    amax = np.abs(w).max(1)
    byte = np.clip(np.where(amax > 0, np.frexp(amax)[1] - 1 + 127 - 7, 1), 1, 254)
    scaled = (w * np.exp2(127.0 - byte)[:, None, :]).reshape(k, n).astype(np.float32)
    words = np.ascontiguousarray(scaled.reshape(k // 512, 128, 4, n).transpose(0, 1, 3, 2)).astype(ml_dtypes.float8_e4m3fn).view(np.uint8)
    return words, np.ascontiguousarray(byte.astype(np.uint8).reshape(k // 512, 16, n))


def unpack_weight(words, scales):
    g, p, n, _ = words.shape
    vals = np.ascontiguousarray(words).view(ml_dtypes.float8_e4m3fn).astype(np.float64) * np.repeat(np.exp2(scales.astype(np.float64) - 127.0), 8, axis=1)[..., None]
    return vals.transpose(0, 1, 3, 2).reshape(g * 512, n)


def sigmoid(v):
    return 1.0 / (1.0 + np.exp(-np.maximum(v, -700.0)))


K, T, S, N, H, J = 512, 2048, 512, 512, 512, 512


def setup_inputs():
    n = np.random.standard_normal
    s = mx_kscale(K)[:, None]
    u = mx_kscale(H)
    packed_xT = pack_weight(n((K, T)) * s)
    return {
        "x_words": packed_xT[0],
        "x_scales": packed_xT[1],
        "w1": (n((K, H)) / np.sqrt(K) / s).astype(np.float32),
        "w2": (n((K, H)) / np.sqrt(K) / s).astype(np.float32),
        "gn": (np.random.uniform(0.5, 1.5, (H, 1)) * u[:, None]).astype(np.float32),
        "w3": (n((H, N)) / np.sqrt(H) / u[:, None]).astype(np.float32),
        "tab": n((N, J)).astype(np.float32),
        "offs": striped(np.random.permutation(T)[:S]),
        "two": striped(np.random.permutation(T)[:S]),
        "n1": striped8(np.stack([np.random.permutation(S) for _ in range(8)])),
        "n2": striped8(np.stack([np.random.permutation(S) for _ in range(8)])),
        "n3": striped8(np.random.randint(0, J, (8, S))),
        "n4": striped8(np.stack([np.random.permutation(S) for _ in range(8)])),
    }


def reference(x_words, x_scales, w1, w2, gn, w3, tab, offs, two, n1, n2, n3, n4):
    xq = unpack_weight(x_words, x_scales)[:, unstriped(offs)]
    y = mxq(f64(w1), 0, "e4m3").T @ xq
    x_two = unpack_weight(x_words, x_scales)[:, unstriped(two)]
    d = mxq(f64(w2), 0, "e4m3").T @ x_two
    z = f64(gn) * (y + (sigmoid(d[np.arange(H)[:, None], runs(n2, H)] - d)) * (y[np.arange(H)[:, None], runs(n1, H)] - y))
    h = mxq(f64(w3), 0, "e4m3").T @ mxq(z, 0, "e4m3")
    return np.maximum(h + f64(tab)[np.arange(N)[:, None], runs(n3, N)], h[np.arange(N)[:, None], runs(n4, N)])

@@ -1,0 +1,205 @@
+from contextlib import ExitStack
+
+import concourse.mybir as mybir
+
+F32 = mybir.dt.float32
+BF16 = mybir.dt.bfloat16
+I32 = mybir.dt.int32
+U32 = mybir.dt.uint32
+U16 = mybir.dt.uint16
+U8 = mybir.dt.uint8
+FP8X4 = mybir.dt.float8_e4m3fn_x4
+ALU = mybir.AluOpType
+ACT = mybir.ActivationFunctionType
+
+P = 128
+PACK = 4
+K, T, S, N, H, J = 512, 2048, 512, 512, 512, 512
+HALF = S // 2
+FLOPS = 3 * 2 * 512 * 512 * 512
+
+
+def tile_picked_twlpullbkind_none_p_kernel(
+    tc, x_words, x_scales, w1, w2, gn, w3, tab, offs, two, n1, n2, n3, n4, out
+):
+    nc = tc.nc
+    with ExitStack() as ctx:
+        lists = ctx.enter_context(tc.tile_pool(name="lists", bufs=1))
+        keep = ctx.enter_context(tc.tile_pool(name="keep", bufs=1))
+        psum = ctx.enter_context(tc.psum_pool(name="psum", bufs=8))
+
+        def load_list(src, name):
+            tile = lists.tile([P, S // 16], U16, name=name)
+            nc.sync.dma_start(tile[:], src)
+            return tile
+
+        def load_rows(src, name, parts):
+            width = src.shape[1] // parts
+            tiles = []
+            for c in range(parts):
+                raw = keep.tile([P, PACK, width], F32, name=f"{name}{c}")
+                nc.sync.dma_start(raw[:], src.rearrange("(p j) c -> p j c", j=PACK)[:, :, c * width : (c + 1) * width])
+                tiles.append(raw)
+            return tiles
+
+        warm = keep.tile([P, 8], F32, name="warm")
+        warm2 = keep.tile([P, 8], F32, name="warm2")
+        xs = keep.tile([P, T], U8, name="xs")
+        nc.vector.memset(xs[:].bitcast(I32), 0)
+        nc.vector.memset(warm[:], 0.0)
+        nc.scalar.activation(warm2[:], warm[:], ACT.Sigmoid)
+
+        two_l = load_list(two, "two_l")
+        for r in range(4):
+            nc.sync.dma_start(xs[32 * r : 32 * r + 4, :].bitcast(I32), x_scales[0, 4 * r : 4 * r + 4, :].bitcast(I32))
+        offs_l = load_list(offs, "offs_l")
+        xw = keep.tile([P, T], U32, name="xw")
+        nc.sync.dma_start(xw[:].bitcast(I32), x_words[0].rearrange("p c r -> p (c r)").bitcast(I32))
+        w2_raw = load_rows(w2, "w2raw", 2)
+        w1_raw = load_rows(w1, "w1raw", 2)
+        n2_l = load_list(n2, "n2_l")
+        n1_l = load_list(n1, "n1_l")
+        gain = keep.tile([P, PACK], F32, name="gain")
+        nc.sync.dma_start(gain[:], gn.rearrange("(p t) o -> p (t o)", t=PACK))
+        w3_raw = load_rows(w3, "w3raw", 1)
+        tab_t = []
+        for t in range(PACK):
+            tile = keep.tile([P, J], F32, name=f"tab{t}")
+            nc.sync.dma_start(tile[:], tab.rearrange("(p t) c -> p t c", t=PACK)[:, t, :])
+            tab_t.append(tile)
+        n3_l = load_list(n3, "n3_l")
+        n4_l = load_list(n4, "n4_l")
+
+        def pick(lst, name):
+            sc = keep.tile([P, S], U8, name=f"{name}_s", align_bytes=64)
+            nc.vector.tensor_copy(sc[:], xs[:].indirect(lst[:]))
+            return sc
+
+        def pickw(lst, name):
+            wd = keep.tile([P, S], U32, name=f"{name}_w", align_bytes=64)
+            nc.vector.tensor_copy(wd[:], xw[:].indirect(lst[:]))
+            return wd
+
+        xb_s = pick(two_l, "xb")
+        xa_s = pick(offs_l, "xa")
+        xb_w = pickw(two_l, "xb")
+        xa_w = pickw(offs_l, "xa")
+
+        def weave(raws, name, engines):
+            g = keep.tile([P, PACK, P, PACK], BF16, name=f"{name}_g", align_bytes=64)
+            mw = P // len(raws)
+            for c, raw in enumerate(raws):
+                dst = g[:, :, c * mw : (c + 1) * mw, :].rearrange("p t m j -> p m j t")
+                src = raw[:].rearrange("p j (m t) -> p m j t", t=PACK)
+                if engines[c] == "v":
+                    nc.vector.tensor_copy(dst, src)
+                else:
+                    nc.scalar.copy(dst, src)
+            return g
+
+        def quant(g, name):
+            codes = keep.tile([P, 512], U32, name=f"{name}_c", align_bytes=64)
+            scales = keep.tile([P, 512], U8, name=f"{name}_q", align_bytes=64)
+            nc.vector.quantize_mx(out=codes[:].bitcast(FP8X4), scales=scales[:], in_=g[:].rearrange("p t m j -> p (t m j)"))
+            return codes, scales
+
+        def product(acc, wq, t, words, scales):
+            cols = slice(P * t, P * (t + 1))
+            nc.tensor.matmul_mx(out=acc, lhsT=wq[0][:, cols].bitcast(FP8X4), lhsT_scale=wq[1][:, cols],
+                                rhs=words.bitcast(FP8X4), rhs_scale=scales, start=True, stop=True)
+
+        w2q = quant(weave(w2_raw, "w2", "sv"), "w2")
+        d_win = []
+        d_cp = keep.tile([P, PACK, S], F32, name="d_cp")
+        y_cp = keep.tile([P, PACK, S], F32, name="y_cp")
+        d_ps = []
+        for t in range(PACK):
+            acc = psum.tile([P, S], F32, name="acc")
+            product(acc[:], w2q, t, xb_w[:], xb_s[:])
+            d_ps.append(acc)
+        w1q = quant(weave(w1_raw, "w1", "vv"), "w1")
+        y_ps = []
+        for t in range(PACK):
+            acc = psum.tile([P, S], F32, name="acc")
+            product(acc[:], w1q, t, xa_w[:], xa_s[:])
+            y_ps.append(acc)
+        y_win = []
+        for t in range(PACK):
+            win = keep.tile([P, S], F32, name=f"dwin{t}")
+            nc.scalar.copy(win[:], d_ps[t][:])
+            nc.scalar.copy(d_cp[:, t, :], d_ps[t][:])
+            d_win.append(win)
+        for t in range(PACK):
+            win = keep.tile([P, S], F32, name=f"ywin{t}")
+            nc.scalar.activation(win[:], y_ps[t][:], ACT.Copy, scale=gain[:, t : t + 1])
+            nc.scalar.activation(y_cp[:, t, :], y_ps[t][:], ACT.Copy, scale=gain[:, t : t + 1])
+            y_win.append(win)
+
+        w3g = weave(w3_raw, "w3", "s")
+
+        h_win = [keep.tile([P, S], F32, name=f"hwin{t}") for t in range(PACK)]
+        u = keep.tile([P, PACK, S], F32, name="u")
+        dd = [keep.tile([P, PACK, HALF], F32, name=f"dd{hf}") for hf in range(2)]
+        sg = [keep.tile([P, PACK, HALF], F32, name=f"sg{hf}") for hf in range(2)]
+        yy = [keep.tile([P, PACK, HALF], F32, name=f"yy{hf}") for hf in range(2)]
+        zp = [keep.tile([P, PACK, HALF], BF16, name=f"zp{hf}") for hf in range(2)]
+        zg = [keep.tile([P, HALF, PACK], BF16, name=f"zg{hf}", align_bytes=64) for hf in range(2)]
+        zc = [keep.tile([P, HALF], U32, name=f"zc{hf}", align_bytes=64) for hf in range(2)]
+        zs = [keep.tile([P, HALF], U8, name=f"zs{hf}", align_bytes=64) for hf in range(2)]
+
+        def cols(hf):
+            return slice(hf * HALF, (hf + 1) * HALF)
+
+        def lcols(hf):
+            return slice(hf * HALF // 16, (hf + 1) * HALF // 16)
+
+        def gate(hf):
+            for t in range(PACK):
+                nc.vector.tensor_tensor(dd[hf][:, t, :], d_win[t][:].indirect(n2_l[:, lcols(hf)]), d_cp[:, t, cols(hf)], ALU.subtract)
+            nc.scalar.activation(sg[hf][:], dd[hf][:], ACT.Sigmoid)
+
+        def pull(hf):
+            for t in range(PACK):
+                nc.vector.tensor_tensor(yy[hf][:, t, :], y_win[t][:].indirect(n1_l[:, lcols(hf)]), y_cp[:, t, cols(hf)], ALU.subtract)
+
+        def mix(hf):
+            nc.vector.tensor_tensor(dd[hf][:], yy[hf][:], sg[hf][:], ALU.mult)
+
+        def mix2(hf):
+            nc.vector.tensor_tensor(zp[hf][:], dd[hf][:], y_cp[:, :, cols(hf)], ALU.add)
+            nc.scalar.copy(zg[hf][:].rearrange("p (c i) t -> p c t i", i=4), zp[hf][:].rearrange("p t (c i) -> p c t i", i=4))
+
+        def second(hf, w3q):
+            nc.vector.quantize_mx(out=zc[hf][:].bitcast(FP8X4), scales=zs[hf][:], in_=zg[hf][:].rearrange("p c t -> p (c t)"))
+            for t in range(PACK):
+                acc = psum.tile([P, S], F32, name="acc")
+                product(acc[:, 0:HALF], w3q, t, zc[hf][:], zs[hf][:])
+                nc.scalar.copy(h_win[t][:, cols(hf)], acc[:, 0:HALF])
+
+        def kind(hf, t):
+            nc.vector.tensor_tensor(u[:, t, cols(hf)], tab_t[t][:].indirect(n3_l[:, lcols(hf)]), h_win[t][:, cols(hf)], ALU.add)
+
+        gate(0)
+        gate(1)
+        pull(0)
+        mix(0)
+        w3q = quant(w3g, "w3")
+        mix2(0)
+        pull(1)
+        second(0, w3q)
+        mix(1)
+        mix2(1)
+        for t in range(2):
+            kind(0, t)
+        second(1, w3q)
+        for t in range(2, PACK):
+            kind(0, t)
+        out_rows = out.rearrange("(p t) c -> p t c", t=PACK)
+        for t in range(PACK):
+            hg = keep.tile([P, S], F32, name=f"hg{t}")
+            res = keep.tile([P, S], F32, name=f"res{t}")
+            nc.vector.tensor_copy(hg[:, cols(0)], h_win[t][:].indirect(n4_l[:, lcols(0)]))
+            kind(1, t)
+            nc.vector.tensor_copy(hg[:, cols(1)], h_win[t][:].indirect(n4_l[:, lcols(1)]))
+            nc.vector.tensor_tensor(res[:], hg[:], u[:, t, :], ALU.max)
+            nc.sync.dma_start(out_rows[:, t, :], res[:])

@@ -1,6 +1,7 @@
 from contextlib import ExitStack
 
 import concourse.mybir as mybir
+from concourse.masks import make_identity
 
 F32 = mybir.dt.float32
 BF16 = mybir.dt.bfloat16
@@ -26,71 +27,67 @@ def tile_picked_twlpullbkind_none_p_kernel(
     with ExitStack() as ctx:
         lists = ctx.enter_context(tc.tile_pool(name="lists", bufs=1))
         keep = ctx.enter_context(tc.tile_pool(name="keep", bufs=1))
-        psum = ctx.enter_context(tc.psum_pool(name="psum", bufs=8))
+        psum = ctx.enter_context(tc.psum_pool(name="psum", bufs=1))
+
+        def sb(shape, dtype, name, tag=None):
+            return keep.tile(shape, dtype, name=name, tag=tag or name, align_bytes=64)
+
+        def bank(i):
+            return psum.tile([P, S], F32, name=f"bank{i}", tag=f"bank{i}")
 
         def load_list(src, name):
             tile = lists.tile([P, S // 16], U16, name=name)
             nc.sync.dma_start(tile[:], src)
             return tile
 
-        def load_rows(src, name, parts):
+        def load_part(src, name, c, parts):
             width = src.shape[1] // parts
-            tiles = []
-            for c in range(parts):
-                raw = keep.tile([P, PACK, width], F32, name=f"{name}{c}")
-                nc.sync.dma_start(raw[:], src.rearrange("(p j) c -> p j c", j=PACK)[:, :, c * width : (c + 1) * width])
-                tiles.append(raw)
-            return tiles
+            raw = sb([P, PACK, width], F32, f"{name}{c}")
+            nc.sync.dma_start(raw[:], src.rearrange("(p j) c -> p j c", j=PACK)[:, :, c * width : (c + 1) * width])
+            return raw
 
-        warm = keep.tile([P, 8], F32, name="warm")
-        warm2 = keep.tile([P, 8], F32, name="warm2")
-        xs = keep.tile([P, T], U8, name="xs")
-        nc.vector.memset(xs[:].bitcast(I32), 0)
+        warm = sb([P, 8], F32, "warm")
+        warm2 = sb([P, 8], F32, "warm2")
+        xs = sb([P, T], U8, "xs")
+        nc.gpsimd.memset(xs[:].bitcast(I32), 0)
         nc.vector.memset(warm[:], 0.0)
         nc.scalar.activation(warm2[:], warm[:], ACT.Sigmoid)
+        ident = sb([P, P], F32, "ident")
+        make_identity(nc, ident[:])
 
         two_l = load_list(two, "two_l")
         for r in range(4):
             nc.sync.dma_start(xs[32 * r : 32 * r + 4, :].bitcast(I32), x_scales[0, 4 * r : 4 * r + 4, :].bitcast(I32))
         offs_l = load_list(offs, "offs_l")
-        xw = keep.tile([P, T], U32, name="xw")
+        xw = sb([P, T], U32, "xw")
+        w2_all = load_part(w2, "w2raw", 0, 1)
+        w2_raw = [w2_all[:, :, 0:256], w2_all[:, :, 256:512]]
         nc.sync.dma_start(xw[:].bitcast(I32), x_words[0].rearrange("p c r -> p (c r)").bitcast(I32))
-        w2_raw = load_rows(w2, "w2raw", 2)
-        w1_raw = load_rows(w1, "w1raw", 2)
+        w1_raw = [load_part(w1, "w1raw", c, 2) for c in range(2)]
         n2_l = load_list(n2, "n2_l")
         n1_l = load_list(n1, "n1_l")
-        gain = keep.tile([P, PACK], F32, name="gain")
+        gain = sb([P, PACK], F32, "gain")
         nc.sync.dma_start(gain[:], gn.rearrange("(p t) o -> p (t o)", t=PACK))
-        w3_raw = load_rows(w3, "w3raw", 1)
+        w3_raw = [load_part(w3, "w3raw", 0, 1)]
         tab_t = []
         for t in range(PACK):
-            tile = keep.tile([P, J], F32, name=f"tab{t}")
+            tile = sb([P, J], F32, f"tab{t}")
             nc.sync.dma_start(tile[:], tab.rearrange("(p t) c -> p t c", t=PACK)[:, t, :])
             tab_t.append(tile)
         n3_l = load_list(n3, "n3_l")
         n4_l = load_list(n4, "n4_l")
 
-        def pick(lst, name):
-            sc = keep.tile([P, S], U8, name=f"{name}_s", align_bytes=64)
-            nc.vector.tensor_copy(sc[:], xs[:].indirect(lst[:]))
-            return sc
+        def pick(table, lst, dtype, name):
+            got = sb([P, S], dtype, name)
+            nc.vector.tensor_copy(got[:], table[:].indirect(lst[:]))
+            return got
 
-        def pickw(lst, name):
-            wd = keep.tile([P, S], U32, name=f"{name}_w", align_bytes=64)
-            nc.vector.tensor_copy(wd[:], xw[:].indirect(lst[:]))
-            return wd
-
-        xb_s = pick(two_l, "xb")
-        xa_s = pick(offs_l, "xa")
-        xb_w = pickw(two_l, "xb")
-        xa_w = pickw(offs_l, "xa")
-
-        def weave(raws, name, engines):
-            g = keep.tile([P, PACK, P, PACK], BF16, name=f"{name}_g", align_bytes=64)
+        def weave(raws, name, engines, tag=None):
+            g = sb([P, PACK, P, PACK], BF16, f"{name}_g", tag)
             mw = P // len(raws)
             for c, raw in enumerate(raws):
                 dst = g[:, :, c * mw : (c + 1) * mw, :].rearrange("p t m j -> p m j t")
-                src = raw[:].rearrange("p j (m t) -> p m j t", t=PACK)
+                src = raw[:, :, :].rearrange("p j (m t) -> p m j t", t=PACK)
                 if engines[c] == "v":
                     nc.vector.tensor_copy(dst, src)
                 else:
@@ -98,8 +95,8 @@ def tile_picked_twlpullbkind_none_p_kernel(
             return g
 
         def quant(g, name):
-            codes = keep.tile([P, 512], U32, name=f"{name}_c", align_bytes=64)
-            scales = keep.tile([P, 512], U8, name=f"{name}_q", align_bytes=64)
+            codes = sb([P, 512], U32, f"{name}_c")
+            scales = sb([P, 512], U8, f"{name}_q")
             nc.vector.quantize_mx(out=codes[:].bitcast(FP8X4), scales=scales[:], in_=g[:].rearrange("p t m j -> p (t m j)"))
             return codes, scales
 
@@ -108,44 +105,12 @@ def tile_picked_twlpullbkind_none_p_kernel(
             nc.tensor.matmul_mx(out=acc, lhsT=wq[0][:, cols].bitcast(FP8X4), lhsT_scale=wq[1][:, cols],
                                 rhs=words.bitcast(FP8X4), rhs_scale=scales, start=True, stop=True)
 
-        w2q = quant(weave(w2_raw, "w2", "sv"), "w2")
-        d_win = []
-        d_cp = keep.tile([P, PACK, S], F32, name="d_cp")
-        y_cp = keep.tile([P, PACK, S], F32, name="y_cp")
-        d_ps = []
-        for t in range(PACK):
-            acc = psum.tile([P, S], F32, name="acc")
-            product(acc[:], w2q, t, xb_w[:], xb_s[:])
-            d_ps.append(acc)
-        w1q = quant(weave(w1_raw, "w1", "vv"), "w1")
-        y_ps = []
-        for t in range(PACK):
-            acc = psum.tile([P, S], F32, name="acc")
-            product(acc[:], w1q, t, xa_w[:], xa_s[:])
-            y_ps.append(acc)
-        y_win = []
-        for t in range(PACK):
-            win = keep.tile([P, S], F32, name=f"dwin{t}")
-            nc.scalar.copy(win[:], d_ps[t][:])
-            nc.scalar.copy(d_cp[:, t, :], d_ps[t][:])
-            d_win.append(win)
-        for t in range(PACK):
-            win = keep.tile([P, S], F32, name=f"ywin{t}")
-            nc.scalar.activation(win[:], y_ps[t][:], ACT.Copy, scale=gain[:, t : t + 1])
-            nc.scalar.activation(y_cp[:, t, :], y_ps[t][:], ACT.Copy, scale=gain[:, t : t + 1])
-            y_win.append(win)
+        def blk(b):
+            return slice(P * b, P * (b + 1))
 
-        w3g = weave(w3_raw, "w3", "s")
-
-        h_win = [keep.tile([P, S], F32, name=f"hwin{t}") for t in range(PACK)]
-        u = keep.tile([P, PACK, S], F32, name="u")
-        dd = [keep.tile([P, PACK, HALF], F32, name=f"dd{hf}") for hf in range(2)]
-        sg = [keep.tile([P, PACK, HALF], F32, name=f"sg{hf}") for hf in range(2)]
-        yy = [keep.tile([P, PACK, HALF], F32, name=f"yy{hf}") for hf in range(2)]
-        zp = [keep.tile([P, PACK, HALF], BF16, name=f"zp{hf}") for hf in range(2)]
-        zg = [keep.tile([P, HALF, PACK], BF16, name=f"zg{hf}", align_bytes=64) for hf in range(2)]
-        zc = [keep.tile([P, HALF], U32, name=f"zc{hf}", align_bytes=64) for hf in range(2)]
-        zs = [keep.tile([P, HALF], U8, name=f"zs{hf}", align_bytes=64) for hf in range(2)]
+        def turn(dst, *srcs):
+            for i, src in enumerate(srcs):
+                nc.tensor.matmul(dst, lhsT=src, rhs=ident[:], is_transpose=True, start=(i == 0), stop=(i == len(srcs) - 1))
 
         def cols(hf):
             return slice(hf * HALF, (hf + 1) * HALF)
@@ -153,53 +118,108 @@ def tile_picked_twlpullbkind_none_p_kernel(
         def lcols(hf):
             return slice(hf * HALF // 16, (hf + 1) * HALF // 16)
 
-        def gate(hf):
-            for t in range(PACK):
-                nc.vector.tensor_tensor(dd[hf][:, t, :], d_win[t][:].indirect(n2_l[:, lcols(hf)]), d_cp[:, t, cols(hf)], ALU.subtract)
-            nc.scalar.activation(sg[hf][:], dd[hf][:], ACT.Sigmoid)
+        xb_s = pick(xs, two_l, U8, "xb_s")
+        xa_s = pick(xs, offs_l, U8, "xa_s")
+        w2q = quant(weave(w2_raw, "w2", "sv"), "w2")
+        xb_w = pick(xw, two_l, U32, "xb_w")
+        xa_w = pick(xw, offs_l, U32, "xa_w")
+        d_ps = []
+        for t in range(PACK):
+            acc = bank(t)
+            product(acc[:], w2q, t, xb_w[:], xb_s[:])
+            d_ps.append(acc)
+        w1q = quant(weave(w1_raw, "w1", "sv"), "w1")
+        y_ps = []
+        for t in range(PACK):
+            acc = bank(4 + t)
+            product(acc[:], w1q, t, xa_w[:], xa_s[:])
+            y_ps.append(acc)
+        d_win, y_win = [], []
+        y_cp = sb([P, PACK, S], F32, "ycp")
+        for t in range(PACK):
+            win = sb([P, 2 * S], F32, f"dwin{t}")
+            nc.scalar.copy(win[:, 0:S], d_ps[t][:])
+            d_win.append(win)
+        for t in range(PACK):
+            win = sb([P, 2 * S], F32, f"ywin{t}")
+            nc.scalar.activation(win[:, 0:S], y_ps[t][:], ACT.Copy, scale=gain[:, t : t + 1])
+            nc.scalar.activation(y_cp[:, t, :], y_ps[t][:], ACT.Copy, scale=gain[:, t : t + 1])
+            y_win.append(win)
 
-        def pull(hf):
-            for t in range(PACK):
-                nc.vector.tensor_tensor(yy[hf][:, t, :], y_win[t][:].indirect(n1_l[:, lcols(hf)]), y_cp[:, t, cols(hf)], ALU.subtract)
+        h_win = [sb([P, 2 * S], F32, f"hwin{t}") for t in range(PACK)]
+        zc = [sb([P, HALF], U32, f"zc{hf}") for hf in range(2)]
+        zs = [sb([P, HALF], U8, f"zs{hf}") for hf in range(2)]
+
+        def probe(ap, name):
+            pr = sb([P, 1], ap.dtype, name)
+            nc.gpsimd.tensor_copy(pr[:], ap)
+
+        ndg0 = sb([P, S], F32, "ndg0")
+        ndg_rest = sb([P, PACK - 1, S], F32, "ndg_rest", "w1_g")
+        ndg = [ndg0[:]] + [ndg_rest[:, t, :] for t in range(PACK - 1)]
+        sT = sb([P, PACK, S], F32, "sT", "gain")
+        for t in range(PACK):
+            nc.vector.tensor_scalar(ndg[t], d_win[t][:].indirect(n2_l[:]), -1.0, 0.0, ALU.mult, ALU.add)
+            acc = bank(t)
+            for b in range(4):
+                turn(acc[:, blk(b)], d_win[t][:, blk(b)], ndg[t][:, blk(b)])
+            nc.scalar.activation(sT[:, t, :], acc[:], ACT.Sigmoid, scale=-1.0)
+        s_ps = {}
+        for hf in range(2):
+            for tp in range(2):
+                acc = bank(4 + 2 * hf + tp)
+                for i in range(4):
+                    turn(acc[:, blk(i)], sT[:, 2 * tp + i // 2, blk(2 * hf + i % 2)])
+                s_ps[hf, tp] = acc
+        pass
+        yy = sb([P, PACK, S], F32, "yy")
+        for t in range(PACK):
+            nc.vector.tensor_tensor(yy[:, t, :], y_win[t][:].indirect(n1_l[:]), y_cp[:, t, :], ALU.subtract)
+        w3g = weave(w3_raw, "w3", "s", "gain")
 
         def mix(hf):
-            nc.vector.tensor_tensor(dd[hf][:], yy[hf][:], sg[hf][:], ALU.mult)
+            mm = sb([P, PACK, HALF], F32, f"mm{hf}")
+            for tp in range(2):
+                nc.vector.tensor_tensor(mm[:, 2 * tp : 2 * tp + 2, :], s_ps[hf, tp][:].rearrange("p (t c) -> p t c", t=2),
+                                        yy[:, 2 * tp : 2 * tp + 2, cols(hf)], ALU.mult)
+            return mm
 
-        def mix2(hf):
-            nc.vector.tensor_tensor(zp[hf][:], dd[hf][:], y_cp[:, :, cols(hf)], ALU.add)
-            nc.scalar.copy(zg[hf][:].rearrange("p (c i) t -> p c t i", i=4), zp[hf][:].rearrange("p t (c i) -> p c t i", i=4))
+        def mix2(hf, mm, tag):
+            zg = sb([P, HALF, PACK], BF16, f"zg{hf}", tag)
+            nc.vector.tensor_tensor(zg[:].rearrange("p (c i) t -> p c t i", i=4), mm[:].rearrange("p t (c i) -> p c t i", i=4),
+                                    y_cp[:, :, cols(hf)].rearrange("p t (c i) -> p c t i", i=4), ALU.add)
+            return zg
 
-        def second(hf, w3q):
-            nc.vector.quantize_mx(out=zc[hf][:].bitcast(FP8X4), scales=zs[hf][:], in_=zg[hf][:].rearrange("p c t -> p (c t)"))
-            for t in range(PACK):
-                acc = psum.tile([P, S], F32, name="acc")
-                product(acc[:, 0:HALF], w3q, t, zc[hf][:], zs[hf][:])
-                nc.scalar.copy(h_win[t][:, cols(hf)], acc[:, 0:HALF])
+        def second(hf, zg, w3q):
+            nc.vector.quantize_mx(out=zc[hf][:].bitcast(FP8X4), scales=zs[hf][:], in_=zg[:].rearrange("p c t -> p (c t)"))
+            for tp in range(2):
+                acc = bank(2 * hf + tp)
+                for i in range(2):
+                    product(acc[:, cols(i)], w3q, 2 * tp + i, zc[hf][:], zs[hf][:])
+                for i in range(2):
+                    nc.scalar.copy(h_win[2 * tp + i][:, cols(hf)], acc[:, cols(i)])
+
+        mm0 = mix(0)
+        mm1 = mix(1)
+        zg0 = mix2(0, mm0, None)
+        w3q = quant(w3g, "w3")
+        second(0, zg0, w3q)
+        zg1 = mix2(1, mm1, "gain")
+        second(1, zg1, w3q)
+        u = [sb([P, PACK, HALF], F32, "u0", "mm1"), sb([P, PACK, HALF], F32, "u1")]
 
         def kind(hf, t):
-            nc.vector.tensor_tensor(u[:, t, cols(hf)], tab_t[t][:].indirect(n3_l[:, lcols(hf)]), h_win[t][:, cols(hf)], ALU.add)
+            nc.vector.tensor_tensor(u[hf][:, t, :], tab_t[t][:].indirect(n3_l[:, lcols(hf)]), h_win[t][:, cols(hf)], ALU.add)
 
-        gate(0)
-        gate(1)
-        pull(0)
-        mix(0)
-        w3q = quant(w3g, "w3")
-        mix2(0)
-        pull(1)
-        second(0, w3q)
-        mix(1)
-        mix2(1)
-        for t in range(2):
-            kind(0, t)
-        second(1, w3q)
-        for t in range(2, PACK):
+        for t in range(PACK):
             kind(0, t)
         out_rows = out.rearrange("(p t) c -> p t c", t=PACK)
+        hg = [sb([P, S], F32, f"hg{t}") for t in range(PACK)]
         for t in range(PACK):
-            hg = keep.tile([P, S], F32, name=f"hg{t}")
-            res = keep.tile([P, S], F32, name=f"res{t}")
-            nc.vector.tensor_copy(hg[:, cols(0)], h_win[t][:].indirect(n4_l[:, lcols(0)]))
             kind(1, t)
-            nc.vector.tensor_copy(hg[:, cols(1)], h_win[t][:].indirect(n4_l[:, lcols(1)]))
-            nc.vector.tensor_tensor(res[:], hg[:], u[:, t, :], ALU.max)
-            nc.sync.dma_start(out_rows[:, t, :], res[:])
+            nc.vector.tensor_copy(hg[t][:], h_win[t][:].indirect(n4_l[:]))
+            for hf in range(2):
+                res = sb([P, HALF], F32, f"res{t}{hf}")
+                nc.vector.tensor_tensor(res[:], hg[t][:, cols(hf)], u[hf][:, t, :], ALU.max)
+                nc.sync.dma_start(out_rows[:, t, cols(hf)], res[:])
+        pass

@@ -157,28 +157,31 @@ def tile_picked_twlpullbkind_none_p_kernel(
         ndg0 = sb([P, S], F32, "ndg0")
         ndg_rest = sb([P, PACK - 1, S], F32, "ndg_rest", "w1_g")
         ndg = [ndg0[:]] + [ndg_rest[:, t, :] for t in range(PACK - 1)]
-        sT = sb([P, PACK, S], F32, "sT", "gain")
+        sT = sb([P, 2, 2, S], F32, "sT", "gain")
+        dd_ps = {(hf, tp): bank(2 * tp + hf) for tp in range(2) for hf in range(2)}
         for t in range(PACK):
             nc.vector.tensor_scalar(ndg[t], d_win[t][:].indirect(n2_l[:]), -1.0, 0.0, ALU.mult, ALU.add)
-            acc = bank(t)
             for b in range(4):
-                turn(acc[:, blk(b)], d_win[t][:, blk(b)], ndg[t][:, blk(b)])
-            nc.scalar.activation(sT[:, t, :], acc[:], ACT.Sigmoid, scale=-1.0)
+                turn(dd_ps[b // 2, t // 2][:, blk(2 * (t % 2) + b % 2)], d_win[t][:, blk(b)], ndg[t][:, blk(b)])
         s_ps = {}
-        for hf in range(2):
+
+        def gate(hf):
             for tp in range(2):
+                nc.scalar.activation(sT[:, hf, tp, :], dd_ps[hf, tp][:], ACT.Sigmoid, scale=-1.0)
                 acc = bank(4 + 2 * hf + tp)
                 for i in range(4):
-                    turn(acc[:, blk(i)], sT[:, 2 * tp + i // 2, blk(2 * hf + i % 2)])
+                    turn(acc[:, blk(i)], sT[:, hf, tp, blk(i)])
                 s_ps[hf, tp] = acc
-        pass
+
+        gate(0)
+        w3g = weave(w3_raw, "w3", "s", "w1_g")
+        gate(1)
         yy = sb([P, PACK, S], F32, "yy")
         for t in range(PACK):
             nc.vector.tensor_tensor(yy[:, t, :], y_win[t][:].indirect(n1_l[:]), y_cp[:, t, :], ALU.subtract)
-        w3g = weave(w3_raw, "w3", "s", "gain")
 
-        def mix(hf):
-            mm = sb([P, PACK, HALF], F32, f"mm{hf}")
+        def mix(hf, tag):
+            mm = sb([P, PACK, HALF], F32, f"mm{hf}", tag)
             for tp in range(2):
                 nc.vector.tensor_tensor(mm[:, 2 * tp : 2 * tp + 2, :], s_ps[hf, tp][:].rearrange("p (t c) -> p t c", t=2),
                                         yy[:, 2 * tp : 2 * tp + 2, cols(hf)], ALU.mult)
@@ -199,17 +202,18 @@ def tile_picked_twlpullbkind_none_p_kernel(
                 for i in range(2):
                     nc.scalar.copy(h_win[2 * tp + i][:, cols(hf)], acc[:, cols(i)])
 
-        mm0 = mix(0)
-        mm1 = mix(1)
-        zg0 = mix2(0, mm0, None)
+        mm0 = mix(0, None)
+        pass
         w3q = quant(w3g, "w3")
+        zg0 = mix2(0, mm0, None)
+        mm1 = mix(1, "w1_g")
         second(0, zg0, w3q)
-        zg1 = mix2(1, mm1, "gain")
+        zg1 = mix2(1, mm1, None)
         second(1, zg1, w3q)
-        u = [sb([P, PACK, HALF], F32, "u0", "mm1"), sb([P, PACK, HALF], F32, "u1")]
+        u = sb([P, PACK, S], F32, "u", "yy")
 
         def kind(hf, t):
-            nc.vector.tensor_tensor(u[hf][:, t, :], tab_t[t][:].indirect(n3_l[:, lcols(hf)]), h_win[t][:, cols(hf)], ALU.add)
+            nc.vector.tensor_tensor(u[:, t, cols(hf)], tab_t[t][:].indirect(n3_l[:, lcols(hf)]), h_win[t][:, cols(hf)], ALU.add)
 
         for t in range(PACK):
             kind(0, t)
@@ -217,9 +221,11 @@ def tile_picked_twlpullbkind_none_p_kernel(
         hg = [sb([P, S], F32, f"hg{t}") for t in range(PACK)]
         for t in range(PACK):
             kind(1, t)
-            nc.vector.tensor_copy(hg[t][:], h_win[t][:].indirect(n4_l[:]))
-            for hf in range(2):
-                res = sb([P, HALF], F32, f"res{t}{hf}")
-                nc.vector.tensor_tensor(res[:], hg[t][:, cols(hf)], u[hf][:, t, :], ALU.max)
-                nc.sync.dma_start(out_rows[:, t, cols(hf)], res[:])
+            pieces = [slice(0, S)] if t < PACK - 1 else [cols(0), cols(1)]
+            for c in pieces:
+                nc.vector.tensor_copy(hg[t][:, c], h_win[t][:].indirect(n4_l[:, c.start // 16 : c.stop // 16]))
+            for i, c in enumerate(pieces):
+                res = sb([P, c.stop - c.start], F32, f"res{t}{i}")
+                nc.vector.tensor_tensor(res[:], hg[t][:, c], u[:, t, c], ALU.max)
+                nc.sync.dma_start(out_rows[:, t, c], res[:])
         pass

from contextlib import ExitStack

import concourse.mybir as mybir
from concourse.masks import make_identity

F32 = mybir.dt.float32
BF16 = mybir.dt.bfloat16
I32 = mybir.dt.int32
U32 = mybir.dt.uint32
U16 = mybir.dt.uint16
U8 = mybir.dt.uint8
FP8X4 = mybir.dt.float8_e4m3fn_x4
ALU = mybir.AluOpType
ACT = mybir.ActivationFunctionType

P = 128
PACK = 4
K, T, S, N, H, J = 512, 2048, 512, 512, 512, 512
HALF = S // 2
FLOPS = 3 * 2 * 512 * 512 * 512


def tile_picked_twlpullbkind_none_p_kernel(
    tc, x_words, x_scales, w1, w2, gn, w3, tab, offs, two, n1, n2, n3, n4, out
):
    nc = tc.nc
    with ExitStack() as ctx:
        lists = ctx.enter_context(tc.tile_pool(name="lists", bufs=1))
        keep = ctx.enter_context(tc.tile_pool(name="keep", bufs=1))
        psum = ctx.enter_context(tc.psum_pool(name="psum", bufs=1))

        def sb(shape, dtype, name, tag=None):
            return keep.tile(shape, dtype, name=name, tag=tag or name, align_bytes=64)

        def bank(i):
            return psum.tile([P, S], F32, name=f"bank{i}", tag=f"bank{i}")

        def load_list(src, name):
            tile = lists.tile([P, S // 16], U16, name=name)
            nc.sync.dma_start(tile[:], src)
            return tile

        def load_part(src, name, c, parts):
            width = src.shape[1] // parts
            raw = sb([P, PACK, width], F32, f"{name}{c}")
            nc.sync.dma_start(raw[:], src.rearrange("(p j) c -> p j c", j=PACK)[:, :, c * width : (c + 1) * width])
            return raw

        warm = sb([P, 8], F32, "warm")
        warm2 = sb([P, 8], F32, "warm2")
        xs = sb([P, T], U8, "xs")
        nc.gpsimd.memset(xs[:].bitcast(I32), 0)
        nc.vector.memset(warm[:], 0.0)
        nc.scalar.activation(warm2[:], warm[:], ACT.Sigmoid)
        ident = sb([P, P], F32, "ident")
        make_identity(nc, ident[:])

        two_l = load_list(two, "two_l")
        for r in range(4):
            nc.sync.dma_start(xs[32 * r : 32 * r + 4, :].bitcast(I32), x_scales[0, 4 * r : 4 * r + 4, :].bitcast(I32))
        offs_l = load_list(offs, "offs_l")
        xw = sb([P, T], U32, "xw")
        w2_all = load_part(w2, "w2raw", 0, 1)
        w2_raw = [w2_all[:, :, 0:256], w2_all[:, :, 256:512]]
        nc.sync.dma_start(xw[:].bitcast(I32), x_words[0].rearrange("p c r -> p (c r)").bitcast(I32))
        w1_raw = [load_part(w1, "w1raw", c, 2) for c in range(2)]
        n2_l = load_list(n2, "n2_l")
        n1_l = load_list(n1, "n1_l")
        gain = sb([P, PACK], F32, "gain")
        nc.sync.dma_start(gain[:], gn.rearrange("(p t) o -> p (t o)", t=PACK))
        w3_raw = [load_part(w3, "w3raw", 0, 1)]
        tab_t = []
        for t in range(PACK):
            tile = sb([P, J], F32, f"tab{t}")
            nc.sync.dma_start(tile[:], tab.rearrange("(p t) c -> p t c", t=PACK)[:, t, :])
            tab_t.append(tile)
        n3_l = load_list(n3, "n3_l")
        n4_l = load_list(n4, "n4_l")

        def pick(table, lst, dtype, name):
            got = sb([P, S], dtype, name)
            nc.vector.tensor_copy(got[:], table[:].indirect(lst[:]))
            return got

        def weave(raws, name, engines, tag=None):
            g = sb([P, PACK, P, PACK], BF16, f"{name}_g", tag)
            mw = P // len(raws)
            for c, raw in enumerate(raws):
                dst = g[:, :, c * mw : (c + 1) * mw, :].rearrange("p t m j -> p m j t")
                src = raw[:, :, :].rearrange("p j (m t) -> p m j t", t=PACK)
                if engines[c] == "v":
                    nc.vector.tensor_copy(dst, src)
                else:
                    nc.scalar.copy(dst, src)
            return g

        def quant(g, name):
            codes = sb([P, 512], U32, f"{name}_c")
            scales = sb([P, 512], U8, f"{name}_q")
            nc.vector.quantize_mx(out=codes[:].bitcast(FP8X4), scales=scales[:], in_=g[:].rearrange("p t m j -> p (t m j)"))
            return codes, scales

        def product(acc, wq, t, words, scales):
            cols = slice(P * t, P * (t + 1))
            nc.tensor.matmul_mx(out=acc, lhsT=wq[0][:, cols].bitcast(FP8X4), lhsT_scale=wq[1][:, cols],
                                rhs=words.bitcast(FP8X4), rhs_scale=scales, start=True, stop=True)

        def blk(b):
            return slice(P * b, P * (b + 1))

        def turn(dst, *srcs):
            for i, src in enumerate(srcs):
                nc.tensor.matmul(dst, lhsT=src, rhs=ident[:], is_transpose=True, start=(i == 0), stop=(i == len(srcs) - 1))

        def cols(hf):
            return slice(hf * HALF, (hf + 1) * HALF)

        def lcols(hf):
            return slice(hf * HALF // 16, (hf + 1) * HALF // 16)

        xb_s = pick(xs, two_l, U8, "xb_s")
        xa_s = pick(xs, offs_l, U8, "xa_s")
        w2q = quant(weave(w2_raw, "w2", "sv"), "w2")
        xb_w = pick(xw, two_l, U32, "xb_w")
        xa_w = pick(xw, offs_l, U32, "xa_w")
        d_ps = []
        for t in range(PACK):
            acc = bank(t)
            product(acc[:], w2q, t, xb_w[:], xb_s[:])
            d_ps.append(acc)
        w1q = quant(weave(w1_raw, "w1", "sv"), "w1")
        y_ps = []
        for t in range(PACK):
            acc = bank(4 + t)
            product(acc[:], w1q, t, xa_w[:], xa_s[:])
            y_ps.append(acc)
        d_win, y_win = [], []
        y_cp = sb([P, PACK, S], F32, "ycp")
        for t in range(PACK):
            win = sb([P, 2 * S], F32, f"dwin{t}")
            nc.scalar.copy(win[:, 0:S], d_ps[t][:])
            d_win.append(win)
        for t in range(PACK):
            win = sb([P, 2 * S], F32, f"ywin{t}")
            nc.scalar.activation(win[:, 0:S], y_ps[t][:], ACT.Copy, scale=gain[:, t : t + 1])
            nc.scalar.activation(y_cp[:, t, :], y_ps[t][:], ACT.Copy, scale=gain[:, t : t + 1])
            y_win.append(win)

        h_win = [sb([P, 2 * S], F32, f"hwin{t}") for t in range(PACK)]
        zc = [sb([P, HALF], U32, f"zc{hf}") for hf in range(2)]
        zs = [sb([P, HALF], U8, f"zs{hf}") for hf in range(2)]

        def probe(ap, name):
            pr = sb([P, 1], ap.dtype, name)
            nc.gpsimd.tensor_copy(pr[:], ap)

        ndg0 = sb([P, S], F32, "ndg0")
        ndg_rest = sb([P, PACK - 1, S], F32, "ndg_rest", "w1_g")
        ndg = [ndg0[:]] + [ndg_rest[:, t, :] for t in range(PACK - 1)]
        sT = sb([P, 2, 2, S], F32, "sT", "gain")
        dd_ps = {(hf, tp): bank(2 * tp + hf) for tp in range(2) for hf in range(2)}
        for t in range(PACK):
            nc.vector.tensor_scalar(ndg[t], d_win[t][:].indirect(n2_l[:]), -1.0, 0.0, ALU.mult, ALU.add)
            for b in range(4):
                turn(dd_ps[b // 2, t // 2][:, blk(2 * (t % 2) + b % 2)], d_win[t][:, blk(b)], ndg[t][:, blk(b)])
        s_ps = {}

        def gate(hf):
            for tp in range(2):
                nc.scalar.activation(sT[:, hf, tp, :], dd_ps[hf, tp][:], ACT.Sigmoid, scale=-1.0)
                acc = bank(4 + 2 * hf + tp)
                for i in range(4):
                    turn(acc[:, blk(i)], sT[:, hf, tp, blk(i)])
                s_ps[hf, tp] = acc

        gate(0)
        w3g = weave(w3_raw, "w3", "s", "w1_g")
        gate(1)
        yy = sb([P, PACK, S], F32, "yy")
        for t in range(PACK):
            nc.vector.tensor_tensor(yy[:, t, :], y_win[t][:].indirect(n1_l[:]), y_cp[:, t, :], ALU.subtract)

        def mix(hf, tag):
            mm = sb([P, PACK, HALF], F32, f"mm{hf}", tag)
            for tp in range(2):
                nc.vector.tensor_tensor(mm[:, 2 * tp : 2 * tp + 2, :], s_ps[hf, tp][:].rearrange("p (t c) -> p t c", t=2),
                                        yy[:, 2 * tp : 2 * tp + 2, cols(hf)], ALU.mult)
            return mm

        def mix2(hf, mm, tag):
            zg = sb([P, HALF, PACK], BF16, f"zg{hf}", tag)
            nc.vector.tensor_tensor(zg[:].rearrange("p (c i) t -> p c t i", i=4), mm[:].rearrange("p t (c i) -> p c t i", i=4),
                                    y_cp[:, :, cols(hf)].rearrange("p t (c i) -> p c t i", i=4), ALU.add)
            return zg

        def second(hf, zg, w3q):
            nc.vector.quantize_mx(out=zc[hf][:].bitcast(FP8X4), scales=zs[hf][:], in_=zg[:].rearrange("p c t -> p (c t)"))
            for tp in range(2):
                acc = bank(2 * hf + tp)
                for i in range(2):
                    product(acc[:, cols(i)], w3q, 2 * tp + i, zc[hf][:], zs[hf][:])
                for i in range(2):
                    nc.scalar.copy(h_win[2 * tp + i][:, cols(hf)], acc[:, cols(i)])

        mm0 = mix(0, None)
        pass
        w3q = quant(w3g, "w3")
        zg0 = mix2(0, mm0, None)
        mm1 = mix(1, "w1_g")
        second(0, zg0, w3q)
        zg1 = mix2(1, mm1, None)
        second(1, zg1, w3q)
        u = sb([P, PACK, S], F32, "u", "yy")

        def kind(hf, t):
            nc.vector.tensor_tensor(u[:, t, cols(hf)], tab_t[t][:].indirect(n3_l[:, lcols(hf)]), h_win[t][:, cols(hf)], ALU.add)

        for t in range(PACK):
            kind(0, t)
        out_rows = out.rearrange("(p t) c -> p t c", t=PACK)
        hg = [sb([P, S], F32, f"hg{t}") for t in range(PACK)]
        for t in range(PACK):
            kind(1, t)
            pieces = [slice(0, S)] if t < PACK - 1 else [cols(0), cols(1)]
            for c in pieces:
                nc.vector.tensor_copy(hg[t][:, c], h_win[t][:].indirect(n4_l[:, c.start // 16 : c.stop // 16]))
            for i, c in enumerate(pieces):
                res = sb([P, c.stop - c.start], F32, f"res{t}{i}")
                nc.vector.tensor_tensor(res[:], hg[t][:, c], u[:, t, c], ALU.max)
                nc.sync.dma_start(out_rows[:, t, c], res[:])
        pass
